import numpy as np
import ml_dtypes

BF16 = ml_dtypes.bfloat16


def bf(x):
    return np.asarray(x, np.float32).astype(BF16)


def f32(x):
    return np.asarray(x, np.float32)


def f64(x):
    return np.asarray(x).astype(np.float64)


def striped(idx):
    return np.tile(idx.reshape(-1, 16).T, (8, 1))


S, K, M, N, V, D = 512, 512, 256, 64, 8, 64


def setup_inputs():
    return {"base": bf(np.random.standard_normal((M, S))), "x": bf(np.random.standard_normal((K, N))), "w": bf(1.5 * np.random.standard_normal((K, M)) / np.sqrt(K)), "offs": striped(np.random.permutation(S)[:N])}


def reference(base, x, w, offs):
    idx = offs[:16].T.reshape(-1)
    z = f64(base).copy()
    z[:, idx] += f64(w).T @ f64(x)
    u = z.reshape(M, V, D)
    u = u - u.max(axis=2, keepdims=True)
    u = np.exp(u)
    u = u / u.sum(axis=2, keepdims=True)
    return u.reshape(M, S)

@@ -1,0 +1,74 @@
+from contextlib import ExitStack
+
+import concourse.mybir as mybir
+from concourse.masks import make_identity
+
+P = 128
+S, K, M, N = 512, 512, 256, 64
+D = 64
+V = S // D
+KB = K // P
+WINDOWS = M // P
+
+BF16, F32, U16 = mybir.dt.bfloat16, mybir.dt.float32, mybir.dt.uint16
+EXP = mybir.ActivationFunctionType.Exp
+SUBTRACT, MULT = mybir.AluOpType.subtract, mybir.AluOpType.mult
+X_AXIS = mybir.AxisListType.X
+
+FLOPS = 2 * K * M * N + 5 * M * S
+
+
+def tile_rows_rescore_kernel(tc, base, x, w, offs, out):
+    nc = tc.nc
+    with ExitStack() as stack:
+        held = stack.enter_context(tc.tile_pool(name="held", bufs=1))
+        work = stack.enter_context(tc.tile_pool(name="work", bufs=WINDOWS))
+        psum = stack.enter_context(tc.psum_pool(name="psum", bufs=1))
+
+        base_sb = held.tile([P, WINDOWS, S], BF16, name="base_sb")
+        nc.sync.dma_start(base_sb[:], base.rearrange("(a p) s -> p a s", p=P))
+        offsets = held.tile([P, N // 16], U16, name="offsets")
+        nc.sync.dma_start(offsets[:], offs)
+        w_sb = held.tile([P, KB, M], BF16, name="w_sb")
+        nc.sync.dma_start(w_sb[:], w.rearrange("(p b) m -> p b m", b=KB))
+        x_sb = held.tile([P, KB, N], BF16, name="x_sb")
+        nc.sync.dma_start(x_sb[:], x.rearrange("(p b) n -> p b n", b=KB))
+
+        identity = held.tile([P, P], BF16, name="identity")
+        make_identity(nc, identity[:])
+
+        windows = [psum.tile([P, S], F32, name=f"window{a}") for a in range(WINDOWS)]
+        for a in range(WINDOWS):
+            nc.tensor.matmul(windows[a][:], identity[:], base_sb[:, a, :], start=True, stop=False)
+
+        for a in range(WINDOWS):
+            for b in range(KB):
+                nc.tensor.matmul(
+                    windows[a][:].indirect(offsets[:]),
+                    w_sb[:, b, a * P : (a + 1) * P],
+                    x_sb[:, b, :],
+                    start=False,
+                    stop=b == KB - 1,
+                )
+
+        for a in range(WINDOWS):
+            slates = windows[a][:].rearrange("p (v d) -> p v d", d=D)
+            largest = work.tile([P, V], F32, name="largest")
+            nc.vector.reduce_max(largest[:], slates, axis=X_AXIS)
+            shifted = work.tile([P, V, D], F32, name="shifted")
+            nc.vector.tensor_tensor(
+                shifted[:], slates, largest[:].unsqueeze(2).to_broadcast([P, V, D]), SUBTRACT
+            )
+            powers = work.tile([P, V, D], F32, name="powers")
+            nc.scalar.activation(powers[:], shifted[:], EXP)
+            total = work.tile([P, V], F32, name="total")
+            nc.vector.reduce_sum(total[:], powers[:], axis=X_AXIS)
+            inverse = work.tile([P, V], F32, name="inverse")
+            nc.vector.reciprocal(inverse[:], total[:])
+            probs = work.tile([P, V, D], F32, name="probs")
+            nc.vector.tensor_tensor(
+                probs[:], powers[:], inverse[:].unsqueeze(2).to_broadcast([P, V, D]), MULT
+            )
+            nc.sync.dma_start(
+                out[a * P : (a + 1) * P, :], probs[:].rearrange("p v d -> p (v d)")
+            )

@@ -7,12 +7,13 @@ P = 128
 S, K, M, N = 512, 512, 256, 64
 D = 64
 V = S // D
+HALF = V // 2
 KB = K // P
 WINDOWS = M // P
 
 BF16, F32, U16 = mybir.dt.bfloat16, mybir.dt.float32, mybir.dt.uint16
 EXP = mybir.ActivationFunctionType.Exp
-SUBTRACT, MULT = mybir.AluOpType.subtract, mybir.AluOpType.mult
+MAX, MULT = mybir.AluOpType.max, mybir.AluOpType.mult
 X_AXIS = mybir.AxisListType.X
 
 FLOPS = 2 * K * M * N + 5 * M * S
@@ -22,7 +23,7 @@ def tile_rows_rescore_kernel(tc, base, x, w, offs, out):
     nc = tc.nc
     with ExitStack() as stack:
         held = stack.enter_context(tc.tile_pool(name="held", bufs=1))
-        work = stack.enter_context(tc.tile_pool(name="work", bufs=WINDOWS))
+        work = stack.enter_context(tc.tile_pool(name="work", bufs=2 * WINDOWS))
         psum = stack.enter_context(tc.psum_pool(name="psum", bufs=1))
 
         base_sb = held.tile([P, WINDOWS, S], BF16, name="base_sb")
@@ -53,22 +54,28 @@ def tile_rows_rescore_kernel(tc, base, x, w, offs, out):
 
         for a in range(WINDOWS):
             slates = windows[a][:].rearrange("p (v d) -> p v d", d=D)
-            largest = work.tile([P, V], F32, name="largest")
-            nc.vector.reduce_max(largest[:], slates, axis=X_AXIS)
-            shifted = work.tile([P, V, D], F32, name="shifted")
-            nc.vector.tensor_tensor(
-                shifted[:], slates, largest[:].unsqueeze(2).to_broadcast([P, V, D]), SUBTRACT
-            )
-            powers = work.tile([P, V, D], F32, name="powers")
-            nc.scalar.activation(powers[:], shifted[:], EXP)
-            total = work.tile([P, V], F32, name="total")
-            nc.vector.reduce_sum(total[:], powers[:], axis=X_AXIS)
-            inverse = work.tile([P, V], F32, name="inverse")
-            nc.vector.reciprocal(inverse[:], total[:])
-            probs = work.tile([P, V, D], F32, name="probs")
-            nc.vector.tensor_tensor(
-                probs[:], powers[:], inverse[:].unsqueeze(2).to_broadcast([P, V, D]), MULT
-            )
-            nc.sync.dma_start(
-                out[a * P : (a + 1) * P, :], probs[:].rearrange("p v d -> p (v d)")
-            )
+            minus_largest = work.tile([P, V], F32, name="minus_largest")
+            nc.vector.tensor_reduce(minus_largest[:], slates, axis=X_AXIS, op=MAX, negate=True)
+            for half in range(2):
+                powers = work.tile([P, HALF, D], F32, name="powers")
+                total = work.tile([P, HALF], F32, name="total")
+                for h in range(HALF):
+                    v = half * HALF + h
+                    nc.scalar.activation(
+                        powers[:, h, :],
+                        slates[:, v, :],
+                        EXP,
+                        bias=minus_largest[:, v : v + 1],
+                        accum_out=total[:, h : h + 1],
+                    )
+                inverse = work.tile([P, HALF], F32, name="inverse")
+                nc.vector.reciprocal(inverse[:], total[:])
+                probs = work.tile([P, HALF, D], F32, name="probs")
+                nc.vector.tensor_tensor(
+                    probs[:], powers[:], inverse[:].unsqueeze(2).to_broadcast([P, HALF, D]), MULT
+                )
+                first = half * HALF * D
+                nc.sync.dma_start(
+                    out[a * P : (a + 1) * P, first : first + HALF * D],
+                    probs[:].rearrange("p v d -> p (v d)"),
+                )

@@ -7,8 +7,10 @@ P = 128
 S, K, M, N = 512, 512, 256, 64
 D = 64
 V = S // D
-HALF = V // 2
+PIECES = 4
+VP = V // PIECES
 KB = K // P
+WARM_UPS = 12
 WINDOWS = M // P
 
 BF16, F32, U16 = mybir.dt.bfloat16, mybir.dt.float32, mybir.dt.uint16
@@ -23,17 +25,24 @@ def tile_rows_rescore_kernel(tc, base, x, w, offs, out):
     nc = tc.nc
     with ExitStack() as stack:
         held = stack.enter_context(tc.tile_pool(name="held", bufs=1))
-        work = stack.enter_context(tc.tile_pool(name="work", bufs=2 * WINDOWS))
+        work = stack.enter_context(tc.tile_pool(name="work", bufs=PIECES * WINDOWS))
         psum = stack.enter_context(tc.psum_pool(name="psum", bufs=1))
 
         base_sb = held.tile([P, WINDOWS, S], BF16, name="base_sb")
-        nc.sync.dma_start(base_sb[:], base.rearrange("(a p) s -> p a s", p=P))
+        for a in range(WINDOWS):
+            nc.sync.dma_start(base_sb[:, a, :], base[a * P : (a + 1) * P, :])
         offsets = held.tile([P, N // 16], U16, name="offsets")
         nc.sync.dma_start(offsets[:], offs)
         w_sb = held.tile([P, KB, M], BF16, name="w_sb")
         nc.sync.dma_start(w_sb[:], w.rearrange("(p b) m -> p b m", b=KB))
         x_sb = held.tile([P, KB, N], BF16, name="x_sb")
         nc.sync.dma_start(x_sb[:], x.rearrange("(p b) n -> p b n", b=KB))
+
+        zeros = held.tile([P, P], BF16, name="zeros")
+        nc.vector.memset(zeros[:], 0.0)
+        spare = psum.tile([P, P], F32, name="spare")
+        for turn in range(WARM_UPS):
+            nc.tensor.matmul(spare[:], zeros[:], zeros[:], start=True, stop=True)
 
         identity = held.tile([P, P], BF16, name="identity")
         make_identity(nc, identity[:])
@@ -56,11 +65,11 @@ def tile_rows_rescore_kernel(tc, base, x, w, offs, out):
             slates = windows[a][:].rearrange("p (v d) -> p v d", d=D)
             minus_largest = work.tile([P, V], F32, name="minus_largest")
             nc.vector.tensor_reduce(minus_largest[:], slates, axis=X_AXIS, op=MAX, negate=True)
-            for half in range(2):
-                powers = work.tile([P, HALF, D], F32, name="powers")
-                total = work.tile([P, HALF], F32, name="total")
-                for h in range(HALF):
-                    v = half * HALF + h
+            for piece in range(PIECES):
+                powers = work.tile([P, VP, D], F32, name="powers")
+                total = work.tile([P, VP], F32, name="total")
+                for h in range(VP):
+                    v = piece * VP + h
                     nc.scalar.activation(
                         powers[:, h, :],
                         slates[:, v, :],
@@ -68,14 +77,14 @@ def tile_rows_rescore_kernel(tc, base, x, w, offs, out):
                         bias=minus_largest[:, v : v + 1],
                         accum_out=total[:, h : h + 1],
                     )
-                inverse = work.tile([P, HALF], F32, name="inverse")
+                inverse = work.tile([P, VP], F32, name="inverse")
                 nc.vector.reciprocal(inverse[:], total[:])
-                probs = work.tile([P, HALF, D], F32, name="probs")
+                probs = work.tile([P, VP, D], F32, name="probs")
                 nc.vector.tensor_tensor(
-                    probs[:], powers[:], inverse[:].unsqueeze(2).to_broadcast([P, HALF, D]), MULT
+                    probs[:], powers[:], inverse[:].unsqueeze(2).to_broadcast([P, VP, D]), MULT
                 )
-                first = half * HALF * D
+                first = piece * VP * D
                 nc.sync.dma_start(
-                    out[a * P : (a + 1) * P, first : first + HALF * D],
+                    out[a * P : (a + 1) * P, first : first + VP * D],
                     probs[:].rearrange("p v d -> p (v d)"),
                 )

from contextlib import ExitStack

import concourse.mybir as mybir
from concourse.masks import make_identity

P = 128
S, K, M, N = 512, 512, 256, 64
D = 64
V = S // D
PIECES = 4
VP = V // PIECES
KB = K // P
WARM_UPS = 12
WINDOWS = M // P

BF16, F32, U16 = mybir.dt.bfloat16, mybir.dt.float32, mybir.dt.uint16
EXP = mybir.ActivationFunctionType.Exp
MAX, MULT = mybir.AluOpType.max, mybir.AluOpType.mult
X_AXIS = mybir.AxisListType.X

FLOPS = 2 * K * M * N + 5 * M * S


def tile_rows_rescore_kernel(tc, base, x, w, offs, out):
    nc = tc.nc
    with ExitStack() as stack:
        held = stack.enter_context(tc.tile_pool(name="held", bufs=1))
        work = stack.enter_context(tc.tile_pool(name="work", bufs=PIECES * WINDOWS))
        psum = stack.enter_context(tc.psum_pool(name="psum", bufs=1))

        base_sb = held.tile([P, WINDOWS, S], BF16, name="base_sb")
        for a in range(WINDOWS):
            nc.sync.dma_start(base_sb[:, a, :], base[a * P : (a + 1) * P, :])
        offsets = held.tile([P, N // 16], U16, name="offsets")
        nc.sync.dma_start(offsets[:], offs)
        w_sb = held.tile([P, KB, M], BF16, name="w_sb")
        nc.sync.dma_start(w_sb[:], w.rearrange("(p b) m -> p b m", b=KB))
        x_sb = held.tile([P, KB, N], BF16, name="x_sb")
        nc.sync.dma_start(x_sb[:], x.rearrange("(p b) n -> p b n", b=KB))

        zeros = held.tile([P, P], BF16, name="zeros")
        nc.vector.memset(zeros[:], 0.0)
        spare = psum.tile([P, P], F32, name="spare")
        for turn in range(WARM_UPS):
            nc.tensor.matmul(spare[:], zeros[:], zeros[:], start=True, stop=True)

        identity = held.tile([P, P], BF16, name="identity")
        make_identity(nc, identity[:])

        windows = [psum.tile([P, S], F32, name=f"window{a}") for a in range(WINDOWS)]
        for a in range(WINDOWS):
            nc.tensor.matmul(windows[a][:], identity[:], base_sb[:, a, :], start=True, stop=False)

        for a in range(WINDOWS):
            for b in range(KB):
                nc.tensor.matmul(
                    windows[a][:].indirect(offsets[:]),
                    w_sb[:, b, a * P : (a + 1) * P],
                    x_sb[:, b, :],
                    start=False,
                    stop=b == KB - 1,
                )

        for a in range(WINDOWS):
            slates = windows[a][:].rearrange("p (v d) -> p v d", d=D)
            minus_largest = work.tile([P, V], F32, name="minus_largest")
            nc.vector.tensor_reduce(minus_largest[:], slates, axis=X_AXIS, op=MAX, negate=True)
            for piece in range(PIECES):
                powers = work.tile([P, VP, D], F32, name="powers")
                total = work.tile([P, VP], F32, name="total")
                for h in range(VP):
                    v = piece * VP + h
                    nc.scalar.activation(
                        powers[:, h, :],
                        slates[:, v, :],
                        EXP,
                        bias=minus_largest[:, v : v + 1],
                        accum_out=total[:, h : h + 1],
                    )
                inverse = work.tile([P, VP], F32, name="inverse")
                nc.vector.reciprocal(inverse[:], total[:])
                probs = work.tile([P, VP, D], F32, name="probs")
                nc.vector.tensor_tensor(
                    probs[:], powers[:], inverse[:].unsqueeze(2).to_broadcast([P, VP, D]), MULT
                )
                first = piece * VP * D
                nc.sync.dma_start(
                    out[a * P : (a + 1) * P, first : first + VP * D],
                    probs[:].rearrange("p v d -> p (v d)"),
                )
